import numpy as np
import ml_dtypes

BF16 = ml_dtypes.bfloat16


def bf(x):
    return np.asarray(x, np.float32).astype(BF16)


def f32(x):
    return np.asarray(x, np.float32)


def f64(x):
    return np.asarray(x).astype(np.float64)


def striped(idx):
    return np.tile(idx.reshape(-1, 16).T, (8, 1))


S, K, M, N, E, Q = 512, 512, 128, 256, 2, 128


def gelu_tanh(v):
    return 0.5 * v * (1.0 + np.tanh(np.sqrt(2.0 / np.pi) * (v + 0.044715 * v**3)))


def setup_inputs():
    return {"base": bf(np.random.standard_normal((M, S))), "x": bf(np.random.standard_normal((K, N))), "w": bf(np.random.standard_normal((E, K, M)) / np.sqrt(K)), "b": f32(0.5 * np.random.standard_normal((M, 1))), "offs": striped(np.random.permutation(S)[:N])}


def reference(base, x, w, b, offs):
    idx = offs[:16].T.reshape(-1)
    z = f64(base).copy()
    for e in range(E):
        z[:, idx[e * Q : (e + 1) * Q]] += f64(w)[e].T @ f64(x)[:, e * Q : (e + 1) * Q]
    return gelu_tanh(z + f64(b))

@@ -1,0 +1,48 @@
+import concourse.mybir as mybir
+from concourse.masks import make_identity
+
+BF16, F32, U16 = mybir.dt.bfloat16, mybir.dt.float32, mybir.dt.uint16
+GELU = mybir.ActivationFunctionType.Gelu_apprx_tanh
+
+P = 128
+M, S = 128, 512
+K, N, E = 512, 256, 2
+Q = N // E
+A = K // P
+
+FLOPS = 2 * K * M * N
+
+
+def tile_scatter_matmul_kernel(tc, base, x, w, b, offs, out):
+    nc = tc.nc
+    with tc.tile_pool(name="held", bufs=1) as held, tc.psum_pool(name="psum", bufs=1) as psum:
+        base_tile = held.tile([P, S], BF16)
+        offsets = held.tile([P, N // 16], U16)
+        w_tile = held.tile([P, E, A * M], BF16)
+        x_tile = held.tile([P, A * N], BF16)
+        bias = held.tile([P, 1], F32)
+        ident = held.tile([P, P], BF16)
+        result = held.tile([P, S], F32)
+        window = psum.tile([P, S], F32)
+
+        nc.sync.dma_start(base_tile[:], base)
+        nc.sync.dma_start(offsets[:], offs)
+        nc.sync.dma_start(w_tile[:], w.rearrange("e (p a) m -> p e (a m)", a=A))
+        nc.sync.dma_start(x_tile[:], x.rearrange("(p a) n -> p (a n)", a=A))
+        nc.sync.dma_start(bias[:], b)
+        make_identity(nc, ident[:])
+
+        nc.tensor.matmul(window[:], ident[:], base_tile[:], start=True, stop=False)
+        for e in range(E):
+            piece = offsets[:, e * Q // 16 : (e + 1) * Q // 16]
+            for a in range(A):
+                nc.tensor.matmul(
+                    window[:].indirect(piece),
+                    w_tile[:, e, a * M : (a + 1) * M],
+                    x_tile[:, a * N + e * Q : a * N + (e + 1) * Q],
+                    start=False,
+                    stop=(e == E - 1 and a == A - 1),
+                )
+
+        nc.scalar.activation(result[:], window[:], GELU, bias=bias[:])
+        nc.sync.dma_start(out, result[:])

@@ -10,6 +10,8 @@ K, N, E = 512, 256, 2
 Q = N // E
 A = K // P
 
+WARM_UPS = 4
+
 FLOPS = 2 * K * M * N
 
 
@@ -24,12 +26,21 @@ def tile_scatter_matmul_kernel(tc, base, x, w, b, offs, out):
         ident = held.tile([P, P], BF16)
         result = held.tile([P, S], F32)
         window = psum.tile([P, S], F32)
+        zeros = held.tile([P, S], BF16)
+        spare = psum.tile([P, S], F32)
+        early = held.tile([P, 1], F32)
 
         nc.sync.dma_start(base_tile[:], base)
         nc.sync.dma_start(offsets[:], offs)
         nc.sync.dma_start(w_tile[:], w.rearrange("e (p a) m -> p e (a m)", a=A))
         nc.sync.dma_start(x_tile[:], x.rearrange("(p a) n -> p (a n)", a=A))
         nc.sync.dma_start(bias[:], b)
+
+        nc.vector.memset(zeros[:], 0.0)
+        for i in range(WARM_UPS):
+            nc.tensor.matmul(spare[:], zeros[:, 0:P], zeros[:], start=True, stop=True)
+        nc.vector.memset(early[:], 0.0)
+        nc.scalar.activation(early[:], early[:], GELU)
         make_identity(nc, ident[:])
 
         nc.tensor.matmul(window[:], ident[:], base_tile[:], start=True, stop=False)

@@ -20,7 +20,7 @@ def tile_scatter_matmul_kernel(tc, base, x, w, b, offs, out):
     with tc.tile_pool(name="held", bufs=1) as held, tc.psum_pool(name="psum", bufs=1) as psum:
         base_tile = held.tile([P, S], BF16)
         offsets = held.tile([P, N // 16], U16)
-        w_tile = held.tile([P, E, A * M], BF16)
+        w_tiles = [held.tile([P, A * M], BF16, name=f"w{e}") for e in range(E)]
         x_tile = held.tile([P, A * N], BF16)
         bias = held.tile([P, 1], F32)
         ident = held.tile([P, P], BF16)
@@ -32,8 +32,9 @@ def tile_scatter_matmul_kernel(tc, base, x, w, b, offs, out):
 
         nc.sync.dma_start(base_tile[:], base)
         nc.sync.dma_start(offsets[:], offs)
-        nc.sync.dma_start(w_tile[:], w.rearrange("e (p a) m -> p e (a m)", a=A))
         nc.sync.dma_start(x_tile[:], x.rearrange("(p a) n -> p (a n)", a=A))
+        for e in range(E):
+            nc.sync.dma_start(w_tiles[e][:], w[e].rearrange("(p a) m -> p (a m)", a=A))
         nc.sync.dma_start(bias[:], b)
 
         nc.vector.memset(zeros[:], 0.0)
@@ -49,7 +50,7 @@ def tile_scatter_matmul_kernel(tc, base, x, w, b, offs, out):
             for a in range(A):
                 nc.tensor.matmul(
                     window[:].indirect(piece),
-                    w_tile[:, e, a * M : (a + 1) * M],
+                    w_tiles[e][:, a * M : (a + 1) * M],
                     x_tile[:, a * N + e * Q : a * N + (e + 1) * Q],
                     start=False,
                     stop=(e == E - 1 and a == A - 1),

@@ -10,7 +10,7 @@ K, N, E = 512, 256, 2
 Q = N // E
 A = K // P
 
-WARM_UPS = 4
+WARM_UPS = 16
 
 FLOPS = 2 * K * M * N
 
@@ -26,8 +26,8 @@ def tile_scatter_matmul_kernel(tc, base, x, w, b, offs, out):
         ident = held.tile([P, P], BF16)
         result = held.tile([P, S], F32)
         window = psum.tile([P, S], F32)
-        zeros = held.tile([P, S], BF16)
-        spare = psum.tile([P, S], F32)
+        zeros = held.tile([P, P], BF16)
+        spare = psum.tile([P, P], F32)
         early = held.tile([P, 1], F32)
 
         nc.sync.dma_start(base_tile[:], base)
@@ -39,7 +39,7 @@ def tile_scatter_matmul_kernel(tc, base, x, w, b, offs, out):
 
         nc.vector.memset(zeros[:], 0.0)
         for i in range(WARM_UPS):
-            nc.tensor.matmul(spare[:], zeros[:, 0:P], zeros[:], start=True, stop=True)
+            nc.tensor.matmul(spare[:], zeros[:], zeros[:], start=True, stop=True)
         nc.vector.memset(early[:], 0.0)
         nc.scalar.activation(early[:], early[:], GELU)
         make_identity(nc, ident[:])
@@ -56,5 +56,7 @@ def tile_scatter_matmul_kernel(tc, base, x, w, b, offs, out):
                     stop=(e == E - 1 and a == A - 1),
                 )
 
-        nc.scalar.activation(result[:], window[:], GELU, bias=bias[:])
-        nc.sync.dma_start(out, result[:])
+        for h in range(2):
+            half = slice(h * S // 2, (h + 1) * S // 2)
+            nc.scalar.activation(result[:, half], window[:, half], GELU, bias=bias[:])
+            nc.sync.dma_start(out[:, half], result[:, half])

import concourse.mybir as mybir
from concourse.masks import make_identity

BF16, F32, U16 = mybir.dt.bfloat16, mybir.dt.float32, mybir.dt.uint16
GELU = mybir.ActivationFunctionType.Gelu_apprx_tanh

P = 128
M, S = 128, 512
K, N, E = 512, 256, 2
Q = N // E
A = K // P

WARM_UPS = 16

FLOPS = 2 * K * M * N


def tile_scatter_matmul_kernel(tc, base, x, w, b, offs, out):
    nc = tc.nc
    with tc.tile_pool(name="held", bufs=1) as held, tc.psum_pool(name="psum", bufs=1) as psum:
        base_tile = held.tile([P, S], BF16)
        offsets = held.tile([P, N // 16], U16)
        w_tiles = [held.tile([P, A * M], BF16, name=f"w{e}") for e in range(E)]
        x_tile = held.tile([P, A * N], BF16)
        bias = held.tile([P, 1], F32)
        ident = held.tile([P, P], BF16)
        result = held.tile([P, S], F32)
        window = psum.tile([P, S], F32)
        zeros = held.tile([P, P], BF16)
        spare = psum.tile([P, P], F32)
        early = held.tile([P, 1], F32)

        nc.sync.dma_start(base_tile[:], base)
        nc.sync.dma_start(offsets[:], offs)
        nc.sync.dma_start(x_tile[:], x.rearrange("(p a) n -> p (a n)", a=A))
        for e in range(E):
            nc.sync.dma_start(w_tiles[e][:], w[e].rearrange("(p a) m -> p (a m)", a=A))
        nc.sync.dma_start(bias[:], b)

        nc.vector.memset(zeros[:], 0.0)
        for i in range(WARM_UPS):
            nc.tensor.matmul(spare[:], zeros[:], zeros[:], start=True, stop=True)
        nc.vector.memset(early[:], 0.0)
        nc.scalar.activation(early[:], early[:], GELU)
        make_identity(nc, ident[:])

        nc.tensor.matmul(window[:], ident[:], base_tile[:], start=True, stop=False)
        for e in range(E):
            piece = offsets[:, e * Q // 16 : (e + 1) * Q // 16]
            for a in range(A):
                nc.tensor.matmul(
                    window[:].indirect(piece),
                    w_tiles[e][:, a * M : (a + 1) * M],
                    x_tile[:, a * N + e * Q : a * N + (e + 1) * Q],
                    start=False,
                    stop=(e == E - 1 and a == A - 1),
                )

        for h in range(2):
            half = slice(h * S // 2, (h + 1) * S // 2)
            nc.scalar.activation(result[:, half], window[:, half], GELU, bias=bias[:])
            nc.sync.dma_start(out[:, half], result[:, half])
